import numpy as np
import ml_dtypes


def mxq(x, axis, fmt="e4m3"):
    dtype, down = {"e4m3": (ml_dtypes.float8_e4m3fn, 7), "e5m2": (ml_dtypes.float8_e5m2, 14)}[fmt]
    v = np.moveaxis(np.asarray(x, np.float32).astype(ml_dtypes.bfloat16).astype(np.float64), axis, -1)
    blocks = v.reshape(v.shape[:-1] + (-1, 32))
    amax = np.abs(blocks).max(-1, keepdims=True)
    byte = np.maximum(np.where(amax > 0, np.frexp(amax)[1] - 1 + 127, 0) - down, 1)
    scale = np.exp2(byte - 127.0)
    codes = (blocks / scale).astype(np.float32).astype(dtype).astype(np.float64)
    return np.moveaxis((codes * scale).reshape(v.shape), -1, axis)


WIDE = False


def mx_kscale(k):
    if not WIDE:
        return np.ones(k)
    levels = np.array([10, -10, 5, -5, 0])
    if k % 512:
        return np.exp2(np.random.permutation(np.resize(levels, k // 32))).repeat(32)
    a = np.empty((k // 512, 16))
    for p in range(k // 512):
        a[p, :8] = np.random.permutation(np.resize(levels, 8))
        for g in range(8):
            far = levels[np.abs(levels - a[p, g]) >= 10]
            a[p, g + 8] = far[np.random.randint(len(far))]
    return np.exp2(a.ravel()).repeat(32)


def f64(x):
    return np.asarray(x).astype(np.float64)


def striped(idx):
    return np.tile(idx.reshape(-1, 16).T, (8, 1)).astype(np.uint16)


def unstriped(offs):
    return offs[:16].T.reshape(-1).astype(np.int64)


def pack_weight(w):
    k, n = w.shape
    w = f64(np.asarray(w, np.float32).astype(ml_dtypes.bfloat16)).reshape(k // 32, 32, n)
    amax = np.abs(w).max(1)
    byte = np.clip(np.where(amax > 0, np.frexp(amax)[1] - 1 + 127 - 7, 1), 1, 254)
    scaled = (w * np.exp2(127.0 - byte)[:, None, :]).reshape(k, n).astype(np.float32)
    words = np.ascontiguousarray(scaled.reshape(k // 512, 128, 4, n).transpose(0, 1, 3, 2)).astype(ml_dtypes.float8_e4m3fn).view(np.uint8)
    return words, np.ascontiguousarray(byte.astype(np.uint8).reshape(k // 512, 16, n))


def unpack_weight(words, scales):
    g, p, n, _ = words.shape
    vals = np.ascontiguousarray(words).view(ml_dtypes.float8_e4m3fn).astype(np.float64) * np.repeat(np.exp2(scales.astype(np.float64) - 127.0), 8, axis=1)[..., None]
    return vals.transpose(0, 1, 3, 2).reshape(g * 512, n)


K, T, S, N, H, W, G, U = 512, 1024, 512, 256, 512, 1024, 2048, 1024


def setup_inputs():
    n = np.random.standard_normal
    s = mx_kscale(K)[:, None]
    u = mx_kscale(H)
    packed_xT = pack_weight(n((K, T)) * s)
    packed_eT = pack_weight(n((K, W)) * s)
    packed_dT = pack_weight(n((K, G)) * s)
    return {
        "x_words": packed_xT[0],
        "x_scales": packed_xT[1],
        "w1": (n((K, H)) / np.sqrt(K) / s).astype(np.float32),
        "e_words": packed_eT[0],
        "e_scales": packed_eT[1],
        "w2": (n((K, H)) / np.sqrt(K) / s).astype(np.float32),
        "d_words": packed_dT[0],
        "d_scales": packed_dT[1],
        "w3": (n((K, H)) / np.sqrt(K) / s).astype(np.float32),
        "unit": (np.random.uniform(0.6, 1.4, (H, 1)) * u[:, None]).astype(np.float32),
        "w4": (n((H, N)) / np.sqrt(H) / u[:, None]).astype(np.float32),
        "offs": striped(np.random.permutation(T)[:S]),
        "prd": striped(np.random.permutation(W)[:S]),
        "obj": striped(np.random.permutation(G)[:S]),
        "ts": striped(np.random.permutation(np.concatenate([np.arange(S), np.random.randint(0, S, U - S)]))),
        "tp": striped(np.random.permutation(np.concatenate([np.arange(S), np.random.randint(0, S, U - S)]))),
        "to": striped(np.random.permutation(np.concatenate([np.arange(S), np.random.randint(0, S, U - S)]))),
    }


def reference(x_words, x_scales, w1, e_words, e_scales, w2, d_words, d_scales, w3, unit, w4, offs, prd, obj, ts, tp, to):
    xq = unpack_weight(x_words, x_scales)[:, unstriped(offs)]
    y = mxq(f64(w1), 0, "e4m3").T @ xq
    sb = y[:, unstriped(ts)]
    e_prd = unpack_weight(e_words, e_scales)[:, unstriped(prd)]
    ye = mxq(f64(w2), 0, "e4m3").T @ e_prd
    pr = ye[:, unstriped(tp)]
    hop = np.maximum(sb * pr, 0.4 * sb)
    d_obj = unpack_weight(d_words, d_scales)[:, unstriped(obj)]
    yd = mxq(f64(w3), 0, "e4m3").T @ d_obj
    ob = yd[:, unstriped(to)]
    hid = f64(unit) * (hop - ob)
    return mxq(f64(w4), 0, "e4m3").T @ mxq(hid, 0, "e4m3")

@@ -1,0 +1,237 @@
+from contextlib import ExitStack
+
+import concourse.mybir as mybir
+
+F32 = mybir.dt.float32
+BF16 = mybir.dt.bfloat16
+I32 = mybir.dt.int32
+U32 = mybir.dt.uint32
+U16 = mybir.dt.uint16
+U8 = mybir.dt.uint8
+FP8X4 = mybir.dt.float8_e4m3fn_x4
+ALU = mybir.AluOpType
+COPY = mybir.ActivationFunctionType.Copy
+
+P = 128
+PACK = 4
+K = 512
+H = 512
+S = 512
+R = 1024
+N = 256
+STRIPE = 16
+SPARE = 16
+CHUNK = 512
+PIECES = ((0, 512), (512, 256), (768, 256))
+
+FLOPS = 2 * (3 * K * H * S + H * N * R)
+
+
+def tile_picked_ytriple_res_p_kernel(
+    tc, x_words, x_scales, w1, e_words, e_scales, w2, d_words, d_scales, w3, unit, w4,
+    offs, prd, obj, ts, tp, to, out,
+):
+    nc = tc.nc
+    with ExitStack() as ctx:
+        keep = ctx.enter_context(tc.tile_pool(name="keep", bufs=1))
+        ring = ctx.enter_context(tc.tile_pool(name="ring", bufs=1))
+        psum = ctx.enter_context(tc.psum_pool(name="psum", bufs=8))
+
+        def load_list(name, src):
+            tile = keep.tile(list(src.shape), U16, name=name)
+            nc.sync.dma_start(tile[:], src)
+            return tile
+
+        def load_words(name, src):
+            tile = keep.tile([P, src.shape[2]], I32, name=name, align_bytes=64)
+            nc.sync.dma_start(tile[:], src[0].rearrange("p n t -> p (n t)").bitcast(I32))
+            return tile
+
+        def load_scales(name, src, queue):
+            tile = keep.tile([P, src.shape[2]], U8, name=name, align_bytes=64)
+            nc.vector.memset(tile[:].bitcast(I32), 0)
+            rows = src[0].rearrange("(q r) n -> r q n", r=4)
+            for r in range(4):
+                queue.dma_start(tile[r:P:32, :].bitcast(I32), rows[r].bitcast(I32))
+            return tile
+
+        def load_weight(name, src, c0, c1):
+            tile = keep.tile([P, PACK, c1 - c0], F32, name=name, tag=name)
+            nc.sync.dma_start(tile[:], src.rearrange("(p j) c -> p j c", j=PACK)[:, :, c0:c1])
+            return tile
+
+        def gather_scales(name, table, lst):
+            tile = keep.tile([P, S], U8, name=name, align_bytes=64)
+            nc.vector.tensor_copy(tile[:], table[:].indirect(lst[:]))
+            return tile
+
+        def gather_words(name, table, lst):
+            tile = keep.tile([P, S], U32, name=name, align_bytes=64)
+            nc.vector.tensor_copy(tile[:], table[:].bitcast(U32).indirect(lst[:]))
+            return tile
+
+        def deal_weight(on_vector, dealt, raw, first, c0, c1):
+            src = raw[:, :, c0 - first : c1 - first].rearrange("p j (m t) -> p m j t", t=PACK)
+            dst = dealt[:].rearrange("p (t m j) -> p m j t", t=PACK, j=PACK)[:, c0 // PACK : c1 // PACK]
+            if on_vector:
+                nc.vector.tensor_copy(dst, src)
+            else:
+                nc.scalar.activation(dst, src, COPY)
+
+        def quantise(name, values, step):
+            cols = values.shape[1] // PACK
+            codes = keep.tile([P, cols], U32, name=name + "_codes", align_bytes=64)
+            scales = keep.tile([P, cols], U8, name=name + "_scales", align_bytes=64)
+            for c in range(0, cols, step):
+                nc.vector.quantize_mx(
+                    out=codes[:, c : c + step].bitcast(FP8X4),
+                    scales=scales[:, c : c + step],
+                    in_=values[:, PACK * c : PACK * (c + step)],
+                )
+            return codes, scales
+
+        def product(weights, t, moving, acc):
+            cols = slice(t * P, (t + 1) * P)
+            nc.tensor.matmul_mx(
+                out=acc,
+                lhsT=weights[0][:, cols].bitcast(FP8X4), lhsT_scale=weights[1][:, cols],
+                rhs=moving[0][:].bitcast(FP8X4), rhs_scale=moving[1][:],
+                start=True, stop=True,
+            )
+
+        def first_products(weights, moving):
+            banks = []
+            for t in range(PACK):
+                bank = psum.tile([P, S], F32, name="bank")
+                product(weights, t, moving, bank[:])
+                banks.append(bank)
+            return banks
+
+        def windows(name):
+            tiles = [keep.tile([P, S + SPARE], F32, name="%s%d" % (name, t)) for t in range(PACK)]
+            for tile in tiles:
+                nc.vector.memset(tile[:, S:], 0.0)
+            return tiles
+
+        def entries(lst, r0, n):
+            return lst[:, r0 // STRIPE : (r0 + n) // STRIPE]
+
+        offs_t = load_list("offs_t", offs)
+        w1_lo = load_weight("w1_lo", w1, 0, H // 2)
+        xw = load_words("xw", x_words)
+        xs = load_scales("xs", x_scales, nc.sync)
+        w1_hi = load_weight("w1_hi", w1, H // 2, H)
+        es = load_scales("es", e_scales, nc.sync)
+        u = keep.tile([P, PACK], F32, name="u")
+        nc.sync.dma_start(u[:], unit.rearrange("(p t) o -> p (t o)", t=PACK))
+        ew = load_words("ew", e_words)
+        prd_t = load_list("prd_t", prd)
+        ts_t = load_list("ts_t", ts)
+        w2_raw = load_weight("w2_raw", w2, 0, H)
+        tp_t = load_list("tp_t", tp)
+        ds = load_scales("ds", d_scales, nc.sync)
+        dw = load_words("dw", d_words)
+        obj_t = load_list("obj_t", obj)
+        w3_raw = load_weight("w3_raw", w3, 0, H)
+        to_t = load_list("to_t", to)
+        w4_raw = load_weight("w4_raw", w4, 0, N)
+        y, ye, yd = windows("y"), windows("ye"), windows("yd")
+
+        w1_b = keep.tile([P, PACK * H], BF16, name="w1_b", align_bytes=64)
+        deal_weight(False, w1_b, w1_lo, 0, 0, 256)
+        xg = (gather_words("xgw", xw, offs_t), gather_scales("xgs", xs, offs_t))
+        deal_weight(False, w1_b, w1_hi, 256, 256, 384)
+        deal_weight(True, w1_b, w1_hi, 256, 384, 512)
+        au = keep.tile([P, PACK], F32, name="au")
+        nc.vector.scalar_tensor_tensor(au[:], u[:], -1.0, u[:], ALU.mult, ALU.max)
+        w1_q = quantise("w1", w1_b, P)
+        y_banks = first_products(w1_q, xg)
+
+        eg = (gather_words("egw", ew, prd_t), gather_scales("egs", es, prd_t))
+        w2_b = keep.tile([P, PACK * H], BF16, name="w2_b", align_bytes=64)
+        deal_weight(True, w2_b, w2_raw, 0, 0, H)
+        w2_q = quantise("w2", w2_b, 2 * P)
+        ye_banks = first_products(w2_q, eg)
+        dg = (gather_words("dgw", dw, obj_t), gather_scales("dgs", ds, obj_t))
+        for t in range(2):
+            nc.vector.tensor_copy(ye[t][:, :S], ye_banks[t][:])
+
+        def subjects(c, t, sb):
+            nc.scalar.activation(sb[:, t, :], y[t][:].indirect(entries(ts_t, c * CHUNK, CHUNK)), COPY)
+            return sb[:, t, :]
+
+        def times_predicate(c, t, sb):
+            prod = ring.tile([P, CHUNK], F32, name="prod", bufs=3)
+            nc.vector.tensor_tensor(prod[:], ye[t][:].indirect(entries(tp_t, c * CHUNK, CHUNK)), sb, ALU.mult)
+            return prod
+
+        hop = [keep.tile([P, PACK, CHUNK], F32, name="hop%d" % c) for c in range(R // CHUNK)]
+
+        def hops(c, sbs):
+            prods = [times_predicate(c, 0, sbs[0])]
+            for t in range(PACK):
+                if t + 1 < PACK:
+                    prods.append(times_predicate(c, t + 1, sbs[t + 1]))
+                nc.vector.scalar_tensor_tensor(hop[c][:, t, :], sbs[t], 0.4, prods[t][:], ALU.mult, ALU.max)
+
+        sb0 = []
+        sb0_t = keep.tile([P, PACK, CHUNK], F32, name="sb0_t")
+        nc.scalar.activation(y[0][:, :S], y_banks[0][:], COPY, scale=au[:, 0:1])
+        for t in range(PACK):
+            if t + 1 < PACK:
+                nc.scalar.activation(y[t + 1][:, :S], y_banks[t + 1][:], COPY, scale=au[:, t + 1 : t + 2])
+            sb0.append(subjects(0, t, sb0_t))
+        for t in range(2, PACK):
+            nc.scalar.activation(ye[t][:, :S], ye_banks[t][:], COPY)
+
+        w3_b = keep.tile([P, PACK * H], BF16, name="w3_b", align_bytes=64)
+        deal_weight(False, w3_b, w3_raw, 0, 0, H)
+        hops(0, sb0)
+        w3_q = quantise("w3", w3_b, H)
+        yd_banks = first_products(w3_q, dg)
+
+        pos = keep.tile([P, PACK], F32, name="pos")
+        nc.gpsimd.tensor_scalar(pos[:], u[:], 0.0, 2.0, ALU.is_ge, ALU.mult)
+        sgn = keep.tile([P, PACK], F32, name="sgn")
+        nc.gpsimd.tensor_scalar(sgn[:], pos[:], 1.0, -1.0, ALU.mult, ALU.add)
+        w4_b = keep.tile([P, PACK * N], BF16, name="w4_b", align_bytes=64)
+        nc.vector.tensor_tensor(
+            w4_b[:].rearrange("p (c i j) -> p c j i", i=4, j=PACK),
+            w4_raw[:].rearrange("p j (c i) -> p c j i", i=4),
+            sgn[:].unsqueeze(1).unsqueeze(3).to_broadcast([P, N // 4, PACK, 4]),
+            ALU.mult,
+        )
+
+        sb1_t = keep.tile([P, PACK, CHUNK], F32, name="sb1_t", tag="w3_raw")
+        sb1 = [subjects(1, t, sb1_t) for t in range(PACK)]
+        for t in range(PACK):
+            nc.scalar.activation(yd[t][:, :S], yd_banks[t][:], COPY, scale=au[:, t : t + 1])
+        hops(1, sb1)
+        w4_q = quantise("w4", w4_b, N)
+
+        out_v = out.rearrange("(h m) r -> m h r", m=P)
+        obs = []
+        for r0, n in PIECES:
+            ob = keep.tile([P, PACK, n], F32, name="ob%d" % r0)
+            for t in range(PACK):
+                nc.scalar.activation(ob[:, t, :], yd[t][:].indirect(entries(to_t, r0, n)), COPY)
+            obs.append(ob)
+        for (r0, n), ob in zip(PIECES, obs):
+            hid = ring.tile([P, PACK * n], BF16, name="hid", align_bytes=64)
+            c, at = divmod(r0, CHUNK)
+            nc.vector.tensor_tensor(
+                hid[:].rearrange("p (c i t) -> p c t i", i=4, t=PACK),
+                hop[c][:, :, at : at + n].rearrange("p t (c i) -> p c t i", i=4),
+                ob[:].rearrange("p t (c i) -> p c t i", i=4),
+                ALU.subtract,
+            )
+            hid_q = quantise("hid%d" % r0, hid, n)
+            for h in range(N // P):
+                bank = psum.tile([P, S], F32, name="bank")
+                product(w4_q, h, hid_q, bank[:, :n])
+                res = keep.tile([P, n], F32, name="res%d_%d" % (r0, h))
+                if h == 0 and r0 + n == R:
+                    nc.vector.tensor_copy(res[:], bank[:, :n])
+                else:
+                    nc.scalar.copy(res[:], bank[:, :n])
+                nc.sync.dma_start(out_v[:, h, r0 : r0 + n], res[:])

@@ -22,7 +22,12 @@ N = 256
 STRIPE = 16
 SPARE = 16
 CHUNK = 512
-PIECES = ((0, 512), (512, 256), (768, 256))
+W3V = 256
+EARLY = 3
+HOLD = 9
+VFROM = 3
+W4S = 0
+PIECES = ((0, 512), (512, 256), (768, 128), (896, 128))
 
 FLOPS = 2 * (3 * K * H * S + H * N * R)
 
@@ -35,7 +40,8 @@ def tile_picked_ytriple_res_p_kernel(
     with ExitStack() as ctx:
         keep = ctx.enter_context(tc.tile_pool(name="keep", bufs=1))
         ring = ctx.enter_context(tc.tile_pool(name="ring", bufs=1))
-        psum = ctx.enter_context(tc.psum_pool(name="psum", bufs=8))
+        shared = ctx.enter_context(tc.tile_pool(name="shared", bufs=1))
+        psum = ctx.enter_context(tc.psum_pool(name="psum", bufs=1))
 
         def load_list(name, src):
             tile = keep.tile(list(src.shape), U16, name=name)
@@ -60,13 +66,13 @@ def tile_picked_ytriple_res_p_kernel(
             nc.sync.dma_start(tile[:], src.rearrange("(p j) c -> p j c", j=PACK)[:, :, c0:c1])
             return tile
 
-        def gather_scales(name, table, lst):
-            tile = keep.tile([P, S], U8, name=name, align_bytes=64)
+        def gather_scales(name, table, lst, pool=keep, offset=None):
+            tile = pool.tile([P, S], U8, name=name, align_bytes=64, offset=offset)
             nc.vector.tensor_copy(tile[:], table[:].indirect(lst[:]))
             return tile
 
-        def gather_words(name, table, lst):
-            tile = keep.tile([P, S], U32, name=name, align_bytes=64)
+        def gather_words(name, table, lst, pool=keep, offset=None):
+            tile = pool.tile([P, S], U32, name=name, align_bytes=64, offset=offset)
             nc.vector.tensor_copy(tile[:], table[:].bitcast(U32).indirect(lst[:]))
             return tile
 
@@ -99,13 +105,10 @@ def tile_picked_ytriple_res_p_kernel(
                 start=True, stop=True,
             )
 
-        def first_products(weights, moving):
-            banks = []
-            for t in range(PACK):
-                bank = psum.tile([P, S], F32, name="bank")
-                product(weights, t, moving, bank[:])
-                banks.append(bank)
-            return banks
+        def first_product(weights, t, moving, b):
+            bank = psum.tile([P, S], F32, name="bank%d" % b)
+            product(weights, t, moving, bank[:])
+            return bank
 
         def windows(name):
             tiles = [keep.tile([P, S + SPARE], F32, name="%s%d" % (name, t)) for t in range(PACK)]
@@ -117,44 +120,44 @@ def tile_picked_ytriple_res_p_kernel(
             return lst[:, r0 // STRIPE : (r0 + n) // STRIPE]
 
         offs_t = load_list("offs_t", offs)
-        w1_lo = load_weight("w1_lo", w1, 0, H // 2)
         xw = load_words("xw", x_words)
         xs = load_scales("xs", x_scales, nc.sync)
+        w1_lo = load_weight("w1_lo", w1, 0, H // 2)
         w1_hi = load_weight("w1_hi", w1, H // 2, H)
-        es = load_scales("es", e_scales, nc.sync)
-        u = keep.tile([P, PACK], F32, name="u")
-        nc.sync.dma_start(u[:], unit.rearrange("(p t) o -> p (t o)", t=PACK))
         ew = load_words("ew", e_words)
         prd_t = load_list("prd_t", prd)
-        ts_t = load_list("ts_t", ts)
+        es = load_scales("es", e_scales, nc.sync)
         w2_raw = load_weight("w2_raw", w2, 0, H)
-        tp_t = load_list("tp_t", tp)
-        ds = load_scales("ds", d_scales, nc.sync)
+        ts_t = load_list("ts_t", ts)
+        u = keep.tile([P, PACK], F32, name="u")
+        nc.sync.dma_start(u[:], unit.rearrange("(p t) o -> p (t o)", t=PACK))
         dw = load_words("dw", d_words)
+        ds = load_scales("ds", d_scales, nc.sync)
         obj_t = load_list("obj_t", obj)
+        tp_t = load_list("tp_t", tp)
         w3_raw = load_weight("w3_raw", w3, 0, H)
         to_t = load_list("to_t", to)
         w4_raw = load_weight("w4_raw", w4, 0, N)
         y, ye, yd = windows("y"), windows("ye"), windows("yd")
 
-        w1_b = keep.tile([P, PACK * H], BF16, name="w1_b", align_bytes=64)
+        w1_b = shared.tile([P, PACK * H], BF16, name="w1_b", align_bytes=64, offset=0)
         deal_weight(False, w1_b, w1_lo, 0, 0, 256)
         xg = (gather_words("xgw", xw, offs_t), gather_scales("xgs", xs, offs_t))
         deal_weight(False, w1_b, w1_hi, 256, 256, 384)
         deal_weight(True, w1_b, w1_hi, 256, 384, 512)
-        au = keep.tile([P, PACK], F32, name="au")
-        nc.vector.scalar_tensor_tensor(au[:], u[:], -1.0, u[:], ALU.mult, ALU.max)
         w1_q = quantise("w1", w1_b, P)
-        y_banks = first_products(w1_q, xg)
+        y_banks = [first_product(w1_q, t, xg, t) for t in range(PACK - 1)]
 
-        eg = (gather_words("egw", ew, prd_t), gather_scales("egs", es, prd_t))
+        eg = (gather_words("egw", ew, prd_t, shared, 0), gather_scales("egs", es, prd_t, shared, 4 * S))
         w2_b = keep.tile([P, PACK * H], BF16, name="w2_b", align_bytes=64)
         deal_weight(True, w2_b, w2_raw, 0, 0, H)
+        au = keep.tile([P, PACK], F32, name="au")
+        nc.vector.scalar_tensor_tensor(au[:], u[:], -1.0, u[:], ALU.mult, ALU.max)
+        au4 = keep.tile([P, PACK], F32, name="au4")
+        nc.gpsimd.tensor_scalar(au4[:], au[:], 0.4, 0.0, ALU.mult, ALU.add)
         w2_q = quantise("w2", w2_b, 2 * P)
-        ye_banks = first_products(w2_q, eg)
+        ye_banks = [first_product(w2_q, t, eg, 3 + t) for t in range(PACK)]
         dg = (gather_words("dgw", dw, obj_t), gather_scales("dgs", ds, obj_t))
-        for t in range(2):
-            nc.vector.tensor_copy(ye[t][:, :S], ye_banks[t][:])
 
         def subjects(c, t, sb):
             nc.scalar.activation(sb[:, t, :], y[t][:].indirect(entries(ts_t, c * CHUNK, CHUNK)), COPY)
@@ -167,57 +170,86 @@ def tile_picked_ytriple_res_p_kernel(
 
         hop = [keep.tile([P, PACK, CHUNK], F32, name="hop%d" % c) for c in range(R // CHUNK)]
 
-        def hops(c, sbs):
-            prods = [times_predicate(c, 0, sbs[0])]
-            for t in range(PACK):
-                if t + 1 < PACK:
-                    prods.append(times_predicate(c, t + 1, sbs[t + 1]))
-                nc.vector.scalar_tensor_tensor(hop[c][:, t, :], sbs[t], 0.4, prods[t][:], ALU.mult, ALU.max)
+        def hops(c, sbs, t0, t1):
+            prods = {t0: times_predicate(c, t0, sbs[t0])}
+            for t in range(t0, t1):
+                if t + 1 < t1:
+                    prods[t + 1] = times_predicate(c, t + 1, sbs[t + 1])
+                nc.vector.scalar_tensor_tensor(hop[c][:, t, :], sbs[t], au4[:, t : t + 1], prods[t][:], ALU.mult, ALU.max)
 
         sb0 = []
         sb0_t = keep.tile([P, PACK, CHUNK], F32, name="sb0_t")
-        nc.scalar.activation(y[0][:, :S], y_banks[0][:], COPY, scale=au[:, 0:1])
-        for t in range(PACK):
-            if t + 1 < PACK:
-                nc.scalar.activation(y[t + 1][:, :S], y_banks[t + 1][:], COPY, scale=au[:, t + 1 : t + 2])
+        def empty(window, bank, t):
+            nc.scalar.activation(window[t][:, :S], bank[:], COPY, scale=au[:, t : t + 1])
+
+        def empty_y(bank, t):
+            nc.scalar.activation(y[t][:, :S], bank[:], COPY)
+
+        empty_y(y_banks[0], 0)
+        for t in range(PACK - 1):
+            if t + 1 < PACK - 1:
+                empty_y(y_banks[t + 1], t + 1)
             sb0.append(subjects(0, t, sb0_t))
-        for t in range(2, PACK):
-            nc.scalar.activation(ye[t][:, :S], ye_banks[t][:], COPY)
+        empty(ye, ye_banks[0], 0)
+        last_bank = first_product(w1_q, PACK - 1, xg, 3)
+        empty(ye, ye_banks[1], 1)
+        empty_y(last_bank, PACK - 1)
+        empty(ye, ye_banks[2], 2)
+        sb0.append(subjects(0, PACK - 1, sb0_t))
+        empty(ye, ye_banks[3], 3)
 
         w3_b = keep.tile([P, PACK * H], BF16, name="w3_b", align_bytes=64)
-        deal_weight(False, w3_b, w3_raw, 0, 0, H)
-        hops(0, sb0)
+        if W3V:
+            deal_weight(True, w3_b, w3_raw, 0, 0, W3V)
+        deal_weight(False, w3_b, w3_raw, 0, W3V, H)
         w3_q = quantise("w3", w3_b, H)
-        yd_banks = first_products(w3_q, dg)
+        yd_banks = [first_product(w3_q, t, dg, (7 + t) % 8) for t in range(PACK)]
+        hops(0, sb0, 0, PACK)
 
         pos = keep.tile([P, PACK], F32, name="pos")
         nc.gpsimd.tensor_scalar(pos[:], u[:], 0.0, 2.0, ALU.is_ge, ALU.mult)
         sgn = keep.tile([P, PACK], F32, name="sgn")
         nc.gpsimd.tensor_scalar(sgn[:], pos[:], 1.0, -1.0, ALU.mult, ALU.add)
         w4_b = keep.tile([P, PACK * N], BF16, name="w4_b", align_bytes=64)
-        nc.vector.tensor_tensor(
-            w4_b[:].rearrange("p (c i j) -> p c j i", i=4, j=PACK),
-            w4_raw[:].rearrange("p j (c i) -> p c j i", i=4),
-            sgn[:].unsqueeze(1).unsqueeze(3).to_broadcast([P, N // 4, PACK, 4]),
-            ALU.mult,
-        )
+        if W4S:
+            sgn_b = keep.tile([P, PACK], BF16, name="sgn_b")
+            nc.gpsimd.tensor_copy(sgn_b[:], sgn[:])
+            w4_p = keep.tile([P, PACK * N], BF16, name="w4_p", align_bytes=64)
+            nc.scalar.activation(
+                w4_p[:].rearrange("p (c i j) -> p c j i", i=4, j=PACK),
+                w4_raw[:].rearrange("p j (c i) -> p c j i", i=4), COPY)
+            nc.vector.tensor_tensor(
+                w4_b[:].rearrange("p (n j) -> p n j", j=PACK),
+                w4_p[:].rearrange("p (n j) -> p n j", j=PACK),
+                sgn_b[:].unsqueeze(1).to_broadcast([P, N, PACK]),
+                ALU.mult,
+            )
+        else:
+            nc.vector.tensor_tensor(
+                w4_b[:].rearrange("p (c i j) -> p c j i", i=4, j=PACK),
+                w4_raw[:].rearrange("p j (c i) -> p c j i", i=4),
+                sgn[:].unsqueeze(1).unsqueeze(3).to_broadcast([P, N // 4, PACK, 4]),
+                ALU.mult,
+            )
 
         sb1_t = keep.tile([P, PACK, CHUNK], F32, name="sb1_t", tag="w3_raw")
         sb1 = [subjects(1, t, sb1_t) for t in range(PACK)]
         for t in range(PACK):
-            nc.scalar.activation(yd[t][:, :S], yd_banks[t][:], COPY, scale=au[:, t : t + 1])
-        hops(1, sb1)
+            empty(yd, yd_banks[t], t)
+        hops(1, sb1, 0, EARLY)
         w4_q = quantise("w4", w4_b, N)
-
         out_v = out.rearrange("(h m) r -> m h r", m=P)
-        obs = []
-        for r0, n in PIECES:
-            ob = keep.tile([P, PACK, n], F32, name="ob%d" % r0)
+
+        def objects(piece, tag):
+            r0, n = PIECES[piece]
+            ob = keep.tile([P, PACK, n], F32, name="ob%d" % r0, tag=tag, align_bytes=64)
             for t in range(PACK):
                 nc.scalar.activation(ob[:, t, :], yd[t][:].indirect(entries(to_t, r0, n)), COPY)
-            obs.append(ob)
-        for (r0, n), ob in zip(PIECES, obs):
-            hid = ring.tile([P, PACK * n], BF16, name="hid", align_bytes=64)
+            return ob
+
+        def hidden(piece, ob):
+            r0, n = PIECES[piece]
+            hid = keep.tile([P, PACK * n], BF16, name="hid%d" % r0, tag="hid%d" % r0, align_bytes=64)
             c, at = divmod(r0, CHUNK)
             nc.vector.tensor_tensor(
                 hid[:].rearrange("p (c i t) -> p c t i", i=4, t=PACK),
@@ -225,13 +257,30 @@ def tile_picked_ytriple_res_p_kernel(
                 ob[:].rearrange("p t (c i) -> p c t i", i=4),
                 ALU.subtract,
             )
+            return hid
+
+        def answers(piece, hid):
+            r0, n = PIECES[piece]
             hid_q = quantise("hid%d" % r0, hid, n)
             for h in range(N // P):
-                bank = psum.tile([P, S], F32, name="bank")
+                bank = psum.tile([P, S], F32, name="bank%d" % ((4 + 2 * piece + h) % 8))
                 product(w4_q, h, hid_q, bank[:, :n])
                 res = keep.tile([P, n], F32, name="res%d_%d" % (r0, h))
-                if h == 0 and r0 + n == R:
+                if h == 0 and piece >= VFROM:
                     nc.vector.tensor_copy(res[:], bank[:, :n])
                 else:
                     nc.scalar.copy(res[:], bank[:, :n])
                 nc.sync.dma_start(out_v[:, h, r0 : r0 + n], res[:])
+
+        obs = [objects(0, "ob0"), objects(1, "ob1")]
+        hid0 = hidden(0, obs[0])
+        if EARLY < PACK:
+            hops(1, sb1, EARLY, PACK)
+        answers(0, hid0)
+        for piece in range(2, len(PIECES)):
+            obs.append(objects(piece, "hid0" if piece == HOLD else "ob%d" % piece))
+        hids = {1: hidden(1, obs[1])}
+        for piece in range(1, len(PIECES)):
+            if piece + 1 < len(PIECES):
+                hids[piece + 1] = hidden(piece + 1, obs[piece + 1])
+            answers(piece, hids[piece])

@@ -1,6 +1,7 @@
 from contextlib import ExitStack
 
 import concourse.mybir as mybir
+from concourse.masks import make_identity
 
 F32 = mybir.dt.float32
 BF16 = mybir.dt.bfloat16
@@ -76,13 +77,16 @@ def tile_picked_ytriple_res_p_kernel(
             nc.vector.tensor_copy(tile[:], table[:].bitcast(U32).indirect(lst[:]))
             return tile
 
-        def deal_weight(on_vector, dealt, raw, first, c0, c1):
-            src = raw[:, :, c0 - first : c1 - first].rearrange("p j (m t) -> p m j t", t=PACK)
-            dst = dealt[:].rearrange("p (t m j) -> p m j t", t=PACK, j=PACK)[:, c0 // PACK : c1 // PACK]
+        def deal_weight(on_vector, dealt, raw, first, t0, t1):
+            groups = raw.shape[2] // 16
+            src = raw[:].rearrange("p j (g t q) -> p t g j q", t=PACK, q=4)
+            dst = dealt[:].rearrange("p (t g q j) -> p t g j q", t=PACK, q=4, j=PACK)
+            dst = dst[:, :, first // 16 : first // 16 + groups]
             if on_vector:
-                nc.vector.tensor_copy(dst, src)
+                nc.vector.tensor_copy(dst[:, t0:t1], src[:, t0:t1])
             else:
-                nc.scalar.activation(dst, src, COPY)
+                for t in range(t0, t1):
+                    nc.scalar.activation(dst[:, t], src[:, t], COPY)
 
         def quantise(name, values, step):
             cols = values.shape[1] // PACK
@@ -129,32 +133,52 @@ def tile_picked_ytriple_res_p_kernel(
         es = load_scales("es", e_scales, nc.sync)
         w2_raw = load_weight("w2_raw", w2, 0, H)
         ts_t = load_list("ts_t", ts)
-        u = keep.tile([P, PACK], F32, name="u")
-        nc.sync.dma_start(u[:], unit.rearrange("(p t) o -> p (t o)", t=PACK))
+        u16 = keep.tile([P, 16], F32, name="u16")
+        nc.sync.dma_start(u16[:], unit.rearrange("(g c) o -> g (c o)", c=16).unsqueeze(1).to_broadcast([P // 4, 4, 16]))
         dw = load_words("dw", d_words)
         ds = load_scales("ds", d_scales, nc.sync)
         obj_t = load_list("obj_t", obj)
         tp_t = load_list("tp_t", tp)
         w3_raw = load_weight("w3_raw", w3, 0, H)
         to_t = load_list("to_t", to)
-        w4_raw = load_weight("w4_raw", w4, 0, N)
+        w4_raw = keep.tile([P, PACK, N], F32, name="w4_raw")
+        w4_rows = w4.rearrange("(g t q) n -> t g q n", t=PACK, q=4)
+        for t in range(PACK):
+            nc.sync.dma_start(w4_raw[:, t, :], w4_rows[t])
         y, ye, yd = windows("y"), windows("ye"), windows("yd")
 
+        eye = keep.tile([P, P], F32, name="eye")
+        make_identity(nc, eye[:])
+        own = keep.tile([P, 4], F32, name="own")
+        nc.vector.tensor_reduce(own[:], eye[:].rearrange("p (g q) -> p q g", q=4), mybir.AxisListType.X, ALU.add)
+        picked = keep.tile([P, PACK, 4], F32, name="picked")
+        nc.gpsimd.tensor_tensor(
+            picked[:], u16[:].rearrange("p (t q) -> p t q", q=4), own[:].unsqueeze(1).to_broadcast([P, PACK, 4]), ALU.mult
+        )
+        pairs = keep.tile([P, PACK, 2], F32, name="pairs")
+        nc.gpsimd.tensor_tensor(pairs[:], picked[:, :, 0:2], picked[:, :, 2:4], ALU.add)
+        u = keep.tile([P, PACK], F32, name="u")
+        nc.gpsimd.tensor_tensor(u[:], pairs[:, :, 0], pairs[:, :, 1], ALU.add)
+        pos = keep.tile([P, PACK], F32, name="pos")
+        nc.gpsimd.tensor_scalar(pos[:], u[:], 0.0, 2.0, ALU.is_ge, ALU.mult)
+        sgn = keep.tile([P, PACK], F32, name="sgn")
+        nc.gpsimd.tensor_scalar(sgn[:], pos[:], 1.0, -1.0, ALU.mult, ALU.add)
+        au = keep.tile([P, PACK], F32, name="au")
+        nc.gpsimd.tensor_tensor(au[:], u[:], sgn[:], ALU.mult)
+        au4 = keep.tile([P, PACK], F32, name="au4")
+        nc.gpsimd.tensor_scalar(au4[:], au[:], 0.4, 0.0, ALU.mult, ALU.add)
+
         w1_b = shared.tile([P, PACK * H], BF16, name="w1_b", align_bytes=64, offset=0)
-        deal_weight(False, w1_b, w1_lo, 0, 0, 256)
+        deal_weight(False, w1_b, w1_lo, 0, 0, PACK)
         xg = (gather_words("xgw", xw, offs_t), gather_scales("xgs", xs, offs_t))
-        deal_weight(False, w1_b, w1_hi, 256, 256, 384)
-        deal_weight(True, w1_b, w1_hi, 256, 384, 512)
+        deal_weight(True, w1_b, w1_hi, H // 2, 0, 2)
+        deal_weight(False, w1_b, w1_hi, H // 2, 2, PACK)
         w1_q = quantise("w1", w1_b, P)
         y_banks = [first_product(w1_q, t, xg, t) for t in range(PACK - 1)]
 
         eg = (gather_words("egw", ew, prd_t, shared, 0), gather_scales("egs", es, prd_t, shared, 4 * S))
         w2_b = keep.tile([P, PACK * H], BF16, name="w2_b", align_bytes=64)
-        deal_weight(True, w2_b, w2_raw, 0, 0, H)
-        au = keep.tile([P, PACK], F32, name="au")
-        nc.vector.scalar_tensor_tensor(au[:], u[:], -1.0, u[:], ALU.mult, ALU.max)
-        au4 = keep.tile([P, PACK], F32, name="au4")
-        nc.gpsimd.tensor_scalar(au4[:], au[:], 0.4, 0.0, ALU.mult, ALU.add)
+        deal_weight(True, w2_b, w2_raw, 0, 0, PACK)
         w2_q = quantise("w2", w2_b, 2 * P)
         ye_banks = [first_product(w2_q, t, eg, 3 + t) for t in range(PACK)]
         dg = (gather_words("dgw", dw, obj_t), gather_scales("dgs", ds, obj_t))
@@ -199,17 +223,12 @@ def tile_picked_ytriple_res_p_kernel(
         empty(ye, ye_banks[3], 3)
 
         w3_b = keep.tile([P, PACK * H], BF16, name="w3_b", align_bytes=64)
-        if W3V:
-            deal_weight(True, w3_b, w3_raw, 0, 0, W3V)
-        deal_weight(False, w3_b, w3_raw, 0, W3V, H)
+        deal_weight(True, w3_b, w3_raw, 0, 0, 2)
+        deal_weight(False, w3_b, w3_raw, 0, 2, PACK)
         w3_q = quantise("w3", w3_b, H)
         yd_banks = [first_product(w3_q, t, dg, (7 + t) % 8) for t in range(PACK)]
         hops(0, sb0, 0, PACK)
 
-        pos = keep.tile([P, PACK], F32, name="pos")
-        nc.gpsimd.tensor_scalar(pos[:], u[:], 0.0, 2.0, ALU.is_ge, ALU.mult)
-        sgn = keep.tile([P, PACK], F32, name="sgn")
-        nc.gpsimd.tensor_scalar(sgn[:], pos[:], 1.0, -1.0, ALU.mult, ALU.add)
         w4_b = keep.tile([P, PACK * N], BF16, name="w4_b", align_bytes=64)
         if W4S:
             sgn_b = keep.tile([P, PACK], BF16, name="sgn_b")

@@ -12,9 +12,12 @@ U8 = mybir.dt.uint8
 FP8X4 = mybir.dt.float8_e4m3fn_x4
 ALU = mybir.AluOpType
 COPY = mybir.ActivationFunctionType.Copy
+LAST_AXIS = mybir.AxisListType.X
 
 P = 128
 PACK = 4
+RUN = 4
+GROUP = PACK * RUN
 K = 512
 H = 512
 S = 512
@@ -23,12 +26,11 @@ N = 256
 STRIPE = 16
 SPARE = 16
 CHUNK = 512
-W3V = 256
-EARLY = 3
-HOLD = 9
-VFROM = 3
-W4S = 0
+BANKS = 8
 PIECES = ((0, 512), (512, 256), (768, 128), (896, 128))
+W1_PLANES_ON_VECTOR = 2
+W3_PLANES_ON_VECTOR = 1
+HOPS_BEFORE_FIRST_PIECE = 3
 
 FLOPS = 2 * (3 * K * H * S + H * N * R)
 
@@ -40,7 +42,7 @@ def tile_picked_ytriple_res_p_kernel(
     nc = tc.nc
     with ExitStack() as ctx:
         keep = ctx.enter_context(tc.tile_pool(name="keep", bufs=1))
-        ring = ctx.enter_context(tc.tile_pool(name="ring", bufs=1))
+        ring = ctx.enter_context(tc.tile_pool(name="ring", bufs=3))
         shared = ctx.enter_context(tc.tile_pool(name="shared", bufs=1))
         psum = ctx.enter_context(tc.psum_pool(name="psum", bufs=1))
 
@@ -51,15 +53,15 @@ def tile_picked_ytriple_res_p_kernel(
 
         def load_words(name, src):
             tile = keep.tile([P, src.shape[2]], I32, name=name, align_bytes=64)
-            nc.sync.dma_start(tile[:], src[0].rearrange("p n t -> p (n t)").bitcast(I32))
+            nc.sync.dma_start(tile[:], src[0].rearrange("p n j -> p (n j)").bitcast(I32))
             return tile
 
-        def load_scales(name, src, queue):
+        def load_scales(name, src):
             tile = keep.tile([P, src.shape[2]], U8, name=name, align_bytes=64)
             nc.vector.memset(tile[:].bitcast(I32), 0)
-            rows = src[0].rearrange("(q r) n -> r q n", r=4)
+            rows = src[0].rearrange("(Q r) n -> r Q n", r=4)
             for r in range(4):
-                queue.dma_start(tile[r:P:32, :].bitcast(I32), rows[r].bitcast(I32))
+                nc.sync.dma_start(tile[r:P:32, :].bitcast(I32), rows[r].bitcast(I32))
             return tile
 
         def load_weight(name, src, c0, c1):
@@ -67,31 +69,37 @@ def tile_picked_ytriple_res_p_kernel(
             nc.sync.dma_start(tile[:], src.rearrange("(p j) c -> p j c", j=PACK)[:, :, c0:c1])
             return tile
 
-        def gather_scales(name, table, lst, pool=keep, offset=None):
-            tile = pool.tile([P, S], U8, name=name, align_bytes=64, offset=offset)
-            nc.vector.tensor_copy(tile[:], table[:].indirect(lst[:]))
-            return tile
+        def gather_words(picked, table, lst):
+            nc.vector.tensor_copy(picked[:], table[:].bitcast(U32).indirect(lst[:]))
 
-        def gather_words(name, table, lst, pool=keep, offset=None):
-            tile = pool.tile([P, S], U32, name=name, align_bytes=64, offset=offset)
-            nc.vector.tensor_copy(tile[:], table[:].bitcast(U32).indirect(lst[:]))
-            return tile
+        def gather_scales(picked, table, lst):
+            nc.vector.tensor_copy(picked[:], table[:].indirect(lst[:]))
 
-        def deal_weight(on_vector, dealt, raw, first, t0, t1):
-            groups = raw.shape[2] // 16
-            src = raw[:].rearrange("p j (g t q) -> p t g j q", t=PACK, q=4)
-            dst = dealt[:].rearrange("p (t g q j) -> p t g j q", t=PACK, q=4, j=PACK)
-            dst = dst[:, :, first // 16 : first // 16 + groups]
-            if on_vector:
-                nc.vector.tensor_copy(dst[:, t0:t1], src[:, t0:t1])
-            else:
-                for t in range(t0, t1):
-                    nc.scalar.activation(dst[:, t], src[:, t], COPY)
+        def gather_table(name, words, scales, lst):
+            picked_words = keep.tile([P, S], U32, name=name + "_words", align_bytes=64)
+            picked_scales = keep.tile([P, S], U8, name=name + "_scales", align_bytes=64)
+            gather_words(picked_words, words, lst)
+            gather_scales(picked_scales, scales, lst)
+            return picked_words, picked_scales
+
+        def deal_views(dealt, raw, first):
+            src = raw[:].rearrange("p j (g t q) -> p t g j q", t=PACK, q=RUN)
+            dst = dealt[:].rearrange("p (t g q j) -> p t g j q", t=PACK, q=RUN, j=PACK)
+            return dst[:, :, first // GROUP : (first + raw.shape[2]) // GROUP], src
+
+        def deal_on_vector(dealt, raw, first, t0, t1):
+            dst, src = deal_views(dealt, raw, first)
+            nc.vector.tensor_copy(dst[:, t0:t1], src[:, t0:t1])
+
+        def deal_on_scalar(dealt, raw, first, t0, t1):
+            dst, src = deal_views(dealt, raw, first)
+            for t in range(t0, t1):
+                nc.scalar.activation(dst[:, t], src[:, t], COPY)
 
         def quantise(name, values, step):
             cols = values.shape[1] // PACK
             codes = keep.tile([P, cols], U32, name=name + "_codes", align_bytes=64)
-            scales = keep.tile([P, cols], U8, name=name + "_scales", align_bytes=64)
+            scales = keep.tile([P, cols], U8, name=name + "_block_scales", align_bytes=64)
             for c in range(0, cols, step):
                 nc.vector.quantize_mx(
                     out=codes[:, c : c + step].bitcast(FP8X4),
@@ -100,19 +108,17 @@ def tile_picked_ytriple_res_p_kernel(
                 )
             return codes, scales
 
-        def product(weights, t, moving, acc):
-            cols = slice(t * P, (t + 1) * P)
+        def product(weights, block, moving, bank_number):
+            cols = slice(block * P, (block + 1) * P)
+            bank = psum.tile([P, S], F32, name="bank%d" % bank_number)
+            acc = bank[:, : moving[0].shape[1]]
             nc.tensor.matmul_mx(
                 out=acc,
                 lhsT=weights[0][:, cols].bitcast(FP8X4), lhsT_scale=weights[1][:, cols],
                 rhs=moving[0][:].bitcast(FP8X4), rhs_scale=moving[1][:],
                 start=True, stop=True,
             )
-
-        def first_product(weights, t, moving, b):
-            bank = psum.tile([P, S], F32, name="bank%d" % b)
-            product(weights, t, moving, bank[:])
-            return bank
+            return acc
 
         def windows(name):
             tiles = [keep.tile([P, S + SPARE], F32, name="%s%d" % (name, t)) for t in range(PACK)]
@@ -120,186 +126,184 @@ def tile_picked_ytriple_res_p_kernel(
                 nc.vector.memset(tile[:, S:], 0.0)
             return tiles
 
-        def entries(lst, r0, n):
-            return lst[:, r0 // STRIPE : (r0 + n) // STRIPE]
+        def entries(lst, first, count):
+            return lst[:, first // STRIPE : (first + count) // STRIPE]
 
         offs_t = load_list("offs_t", offs)
-        xw = load_words("xw", x_words)
-        xs = load_scales("xs", x_scales, nc.sync)
+        x_w = load_words("x_w", x_words)
+        x_s = load_scales("x_s", x_scales)
         w1_lo = load_weight("w1_lo", w1, 0, H // 2)
         w1_hi = load_weight("w1_hi", w1, H // 2, H)
-        ew = load_words("ew", e_words)
+        e_w = load_words("e_w", e_words)
         prd_t = load_list("prd_t", prd)
-        es = load_scales("es", e_scales, nc.sync)
+        e_s = load_scales("e_s", e_scales)
         w2_raw = load_weight("w2_raw", w2, 0, H)
         ts_t = load_list("ts_t", ts)
-        u16 = keep.tile([P, 16], F32, name="u16")
-        nc.sync.dma_start(u16[:], unit.rearrange("(g c) o -> g (c o)", c=16).unsqueeze(1).to_broadcast([P // 4, 4, 16]))
-        dw = load_words("dw", d_words)
-        ds = load_scales("ds", d_scales, nc.sync)
+        unit_group = keep.tile([P, GROUP], F32, name="unit_group")
+        nc.sync.dma_start(
+            unit_group[:],
+            unit.rearrange("(g c) o -> g (c o)", c=GROUP).unsqueeze(1).to_broadcast([P // RUN, RUN, GROUP]),
+        )
+        d_w = load_words("d_w", d_words)
+        d_s = load_scales("d_s", d_scales)
         obj_t = load_list("obj_t", obj)
         tp_t = load_list("tp_t", tp)
         w3_raw = load_weight("w3_raw", w3, 0, H)
         to_t = load_list("to_t", to)
         w4_raw = keep.tile([P, PACK, N], F32, name="w4_raw")
-        w4_rows = w4.rearrange("(g t q) n -> t g q n", t=PACK, q=4)
+        w4_rows = w4.rearrange("(g t q) n -> t g q n", t=PACK, q=RUN)
         for t in range(PACK):
             nc.sync.dma_start(w4_raw[:, t, :], w4_rows[t])
         y, ye, yd = windows("y"), windows("ye"), windows("yd")
 
         eye = keep.tile([P, P], F32, name="eye")
         make_identity(nc, eye[:])
-        own = keep.tile([P, 4], F32, name="own")
-        nc.vector.tensor_reduce(own[:], eye[:].rearrange("p (g q) -> p q g", q=4), mybir.AxisListType.X, ALU.add)
-        picked = keep.tile([P, PACK, 4], F32, name="picked")
-        nc.gpsimd.tensor_tensor(
-            picked[:], u16[:].rearrange("p (t q) -> p t q", q=4), own[:].unsqueeze(1).to_broadcast([P, PACK, 4]), ALU.mult
+        own = keep.tile([P, RUN], F32, name="own")
+        nc.vector.tensor_reduce(own[:], eye[:].rearrange("p (g q) -> p q g", q=RUN), LAST_AXIS, ALU.add)
+        masked = keep.tile([P, PACK, RUN], F32, name="masked")
+        nc.vector.tensor_tensor(
+            masked[:],
+            unit_group[:].rearrange("p (t q) -> p t q", q=RUN),
+            own[:].unsqueeze(1).to_broadcast([P, PACK, RUN]),
+            ALU.mult,
         )
-        pairs = keep.tile([P, PACK, 2], F32, name="pairs")
-        nc.gpsimd.tensor_tensor(pairs[:], picked[:, :, 0:2], picked[:, :, 2:4], ALU.add)
-        u = keep.tile([P, PACK], F32, name="u")
-        nc.gpsimd.tensor_tensor(u[:], pairs[:, :, 0], pairs[:, :, 1], ALU.add)
-        pos = keep.tile([P, PACK], F32, name="pos")
-        nc.gpsimd.tensor_scalar(pos[:], u[:], 0.0, 2.0, ALU.is_ge, ALU.mult)
-        sgn = keep.tile([P, PACK], F32, name="sgn")
-        nc.gpsimd.tensor_scalar(sgn[:], pos[:], 1.0, -1.0, ALU.mult, ALU.add)
-        au = keep.tile([P, PACK], F32, name="au")
-        nc.gpsimd.tensor_tensor(au[:], u[:], sgn[:], ALU.mult)
-        au4 = keep.tile([P, PACK], F32, name="au4")
-        nc.gpsimd.tensor_scalar(au4[:], au[:], 0.4, 0.0, ALU.mult, ALU.add)
+        size = keep.tile([P, PACK], F32, name="size")
+        nc.vector.tensor_reduce(size[:], masked[:], LAST_AXIS, ALU.max, apply_absolute_value=True)
+        floor_factor = keep.tile([P, PACK], F32, name="floor_factor")
+        nc.vector.tensor_scalar(floor_factor[:], size[:], 0.4, None, ALU.mult)
+        halves = keep.tile([P, PACK, RUN // 2], F32, name="halves")
+        nc.gpsimd.tensor_tensor(halves[:], masked[:, :, : RUN // 2], masked[:, :, RUN // 2 :], ALU.add)
+        signed = keep.tile([P, PACK], F32, name="signed")
+        nc.gpsimd.tensor_tensor(signed[:], halves[:, :, 0], halves[:, :, 1], ALU.add)
+        twice_positive = keep.tile([P, PACK], F32, name="twice_positive")
+        nc.gpsimd.tensor_scalar(twice_positive[:], signed[:], 0.0, 2.0, ALU.is_ge, ALU.mult)
+        sign = keep.tile([P, PACK], F32, name="sign")
+        nc.gpsimd.tensor_scalar(sign[:], twice_positive[:], 1.0, -1.0, ALU.mult, ALU.add)
 
-        w1_b = shared.tile([P, PACK * H], BF16, name="w1_b", align_bytes=64, offset=0)
-        deal_weight(False, w1_b, w1_lo, 0, 0, PACK)
-        xg = (gather_words("xgw", xw, offs_t), gather_scales("xgs", xs, offs_t))
-        deal_weight(True, w1_b, w1_hi, H // 2, 0, 2)
-        deal_weight(False, w1_b, w1_hi, H // 2, 2, PACK)
-        w1_q = quantise("w1", w1_b, P)
-        y_banks = [first_product(w1_q, t, xg, t) for t in range(PACK - 1)]
+        w1_dealt = shared.tile([P, PACK * H], BF16, name="w1_dealt", align_bytes=64, offset=0)
+        deal_on_scalar(w1_dealt, w1_lo, 0, 0, PACK)
+        x_picked = gather_table("x_picked", x_w, x_s, offs_t)
+        deal_on_vector(w1_dealt, w1_hi, H // 2, 0, W1_PLANES_ON_VECTOR)
+        deal_on_scalar(w1_dealt, w1_hi, H // 2, W1_PLANES_ON_VECTOR, PACK)
+        w1_q = quantise("w1", w1_dealt, P)
+        last = PACK - 1
+        y_acc = [product(w1_q, t, x_picked, t) for t in range(last)]
 
-        eg = (gather_words("egw", ew, prd_t, shared, 0), gather_scales("egs", es, prd_t, shared, 4 * S))
-        w2_b = keep.tile([P, PACK * H], BF16, name="w2_b", align_bytes=64)
-        deal_weight(True, w2_b, w2_raw, 0, 0, PACK)
-        w2_q = quantise("w2", w2_b, 2 * P)
-        ye_banks = [first_product(w2_q, t, eg, 3 + t) for t in range(PACK)]
-        dg = (gather_words("dgw", dw, obj_t), gather_scales("dgs", ds, obj_t))
+        e_picked = (
+            shared.tile([P, S], U32, name="e_picked_words", align_bytes=64, offset=0),
+            shared.tile([P, S], U8, name="e_picked_scales", align_bytes=64, offset=4 * S),
+        )
+        gather_words(e_picked[0], e_w, prd_t)
+        gather_scales(e_picked[1], e_s, prd_t)
+        w2_dealt = keep.tile([P, PACK * H], BF16, name="w2_dealt", align_bytes=64)
+        deal_on_vector(w2_dealt, w2_raw, 0, 0, PACK)
+        w2_q = quantise("w2", w2_dealt, 2 * P)
+        ye_acc = [product(w2_q, t, e_picked, last + t) for t in range(PACK)]
+        d_picked = gather_table("d_picked", d_w, d_s, obj_t)
 
-        def subjects(c, t, sb):
+        def empty(window, acc):
+            nc.scalar.activation(window[:, :S], acc, COPY)
+
+        def empty_scaled(window, acc, t):
+            nc.scalar.activation(window[:, :S], acc, COPY, scale=size[:, t : t + 1])
+
+        def fetch_subjects(sb, c, t):
             nc.scalar.activation(sb[:, t, :], y[t][:].indirect(entries(ts_t, c * CHUNK, CHUNK)), COPY)
-            return sb[:, t, :]
 
-        def times_predicate(c, t, sb):
-            prod = ring.tile([P, CHUNK], F32, name="prod", bufs=3)
-            nc.vector.tensor_tensor(prod[:], ye[t][:].indirect(entries(tp_t, c * CHUNK, CHUNK)), sb, ALU.mult)
+        def times_predicate(sb, c, t):
+            prod = ring.tile([P, CHUNK], F32, name="prod")
+            nc.vector.tensor_tensor(
+                prod[:], ye[t][:].indirect(entries(tp_t, c * CHUNK, CHUNK)), sb[:, t, :], ALU.mult
+            )
             return prod
 
         hop = [keep.tile([P, PACK, CHUNK], F32, name="hop%d" % c) for c in range(R // CHUNK)]
 
-        def hops(c, sbs, t0, t1):
-            prods = {t0: times_predicate(c, t0, sbs[t0])}
+        def hops(sb, c, t0, t1):
+            prods = {t0: times_predicate(sb, c, t0)}
             for t in range(t0, t1):
                 if t + 1 < t1:
-                    prods[t + 1] = times_predicate(c, t + 1, sbs[t + 1])
-                nc.vector.scalar_tensor_tensor(hop[c][:, t, :], sbs[t], au4[:, t : t + 1], prods[t][:], ALU.mult, ALU.max)
+                    prods[t + 1] = times_predicate(sb, c, t + 1)
+                nc.vector.scalar_tensor_tensor(
+                    hop[c][:, t, :], sb[:, t, :], floor_factor[:, t : t + 1], prods[t][:], ALU.mult, ALU.max
+                )
 
-        sb0 = []
-        sb0_t = keep.tile([P, PACK, CHUNK], F32, name="sb0_t")
-        def empty(window, bank, t):
-            nc.scalar.activation(window[t][:, :S], bank[:], COPY, scale=au[:, t : t + 1])
+        sb0 = keep.tile([P, PACK, CHUNK], F32, name="sb0")
+        empty(y[0], y_acc[0])
+        for t in range(last):
+            if t + 1 < last:
+                empty(y[t + 1], y_acc[t + 1])
+            fetch_subjects(sb0, 0, t)
+        empty_scaled(ye[0], ye_acc[0], 0)
+        y_last_acc = product(w1_q, last, x_picked, last)
+        empty_scaled(ye[1], ye_acc[1], 1)
+        empty(y[last], y_last_acc)
+        empty_scaled(ye[2], ye_acc[2], 2)
+        fetch_subjects(sb0, 0, last)
+        empty_scaled(ye[3], ye_acc[3], 3)
 
-        def empty_y(bank, t):
-            nc.scalar.activation(y[t][:, :S], bank[:], COPY)
+        w3_dealt = keep.tile([P, PACK * H], BF16, name="w3_dealt", align_bytes=64)
+        deal_on_vector(w3_dealt, w3_raw, 0, 0, W3_PLANES_ON_VECTOR)
+        deal_on_scalar(w3_dealt, w3_raw, 0, W3_PLANES_ON_VECTOR, PACK)
+        w3_q = quantise("w3", w3_dealt, H)
+        yd_acc = [product(w3_q, t, d_picked, (BANKS - 1 + t) % BANKS) for t in range(PACK)]
+        hops(sb0, 0, 0, PACK)
 
-        empty_y(y_banks[0], 0)
-        for t in range(PACK - 1):
-            if t + 1 < PACK - 1:
-                empty_y(y_banks[t + 1], t + 1)
-            sb0.append(subjects(0, t, sb0_t))
-        empty(ye, ye_banks[0], 0)
-        last_bank = first_product(w1_q, PACK - 1, xg, 3)
-        empty(ye, ye_banks[1], 1)
-        empty_y(last_bank, PACK - 1)
-        empty(ye, ye_banks[2], 2)
-        sb0.append(subjects(0, PACK - 1, sb0_t))
-        empty(ye, ye_banks[3], 3)
+        w4_signed = keep.tile([P, PACK * N], BF16, name="w4_signed", align_bytes=64)
+        nc.vector.tensor_tensor(
+            w4_signed[:].rearrange("p (c q t) -> p c t q", q=RUN, t=PACK),
+            w4_raw[:].rearrange("p t (c q) -> p c t q", q=RUN),
+            sign[:].unsqueeze(1).unsqueeze(3).to_broadcast([P, N // RUN, PACK, RUN]),
+            ALU.mult,
+        )
 
-        w3_b = keep.tile([P, PACK * H], BF16, name="w3_b", align_bytes=64)
-        deal_weight(True, w3_b, w3_raw, 0, 0, 2)
-        deal_weight(False, w3_b, w3_raw, 0, 2, PACK)
-        w3_q = quantise("w3", w3_b, H)
-        yd_banks = [first_product(w3_q, t, dg, (7 + t) % 8) for t in range(PACK)]
-        hops(0, sb0, 0, PACK)
-
-        w4_b = keep.tile([P, PACK * N], BF16, name="w4_b", align_bytes=64)
-        if W4S:
-            sgn_b = keep.tile([P, PACK], BF16, name="sgn_b")
-            nc.gpsimd.tensor_copy(sgn_b[:], sgn[:])
-            w4_p = keep.tile([P, PACK * N], BF16, name="w4_p", align_bytes=64)
-            nc.scalar.activation(
-                w4_p[:].rearrange("p (c i j) -> p c j i", i=4, j=PACK),
-                w4_raw[:].rearrange("p j (c i) -> p c j i", i=4), COPY)
-            nc.vector.tensor_tensor(
-                w4_b[:].rearrange("p (n j) -> p n j", j=PACK),
-                w4_p[:].rearrange("p (n j) -> p n j", j=PACK),
-                sgn_b[:].unsqueeze(1).to_broadcast([P, N, PACK]),
-                ALU.mult,
-            )
-        else:
-            nc.vector.tensor_tensor(
-                w4_b[:].rearrange("p (c i j) -> p c j i", i=4, j=PACK),
-                w4_raw[:].rearrange("p j (c i) -> p c j i", i=4),
-                sgn[:].unsqueeze(1).unsqueeze(3).to_broadcast([P, N // 4, PACK, 4]),
-                ALU.mult,
-            )
-
-        sb1_t = keep.tile([P, PACK, CHUNK], F32, name="sb1_t", tag="w3_raw")
-        sb1 = [subjects(1, t, sb1_t) for t in range(PACK)]
+        sb1 = keep.tile([P, PACK, CHUNK], F32, name="sb1", tag="w3_raw")
         for t in range(PACK):
-            empty(yd, yd_banks[t], t)
-        hops(1, sb1, 0, EARLY)
-        w4_q = quantise("w4", w4_b, N)
-        out_v = out.rearrange("(h m) r -> m h r", m=P)
+            fetch_subjects(sb1, 1, t)
+        for t in range(PACK):
+            empty_scaled(yd[t], yd_acc[t], t)
+        hops(sb1, 1, 0, HOPS_BEFORE_FIRST_PIECE)
+        w4_q = quantise("w4", w4_signed, N)
 
-        def objects(piece, tag):
-            r0, n = PIECES[piece]
-            ob = keep.tile([P, PACK, n], F32, name="ob%d" % r0, tag=tag, align_bytes=64)
+        ob = []
+        for first, count in PIECES:
+            fetched = keep.tile([P, PACK, count], F32, name="ob%d" % first)
             for t in range(PACK):
-                nc.scalar.activation(ob[:, t, :], yd[t][:].indirect(entries(to_t, r0, n)), COPY)
-            return ob
+                nc.scalar.activation(fetched[:, t, :], yd[t][:].indirect(entries(to_t, first, count)), COPY)
+            ob.append(fetched)
 
-        def hidden(piece, ob):
-            r0, n = PIECES[piece]
-            hid = keep.tile([P, PACK * n], BF16, name="hid%d" % r0, tag="hid%d" % r0, align_bytes=64)
-            c, at = divmod(r0, CHUNK)
+        def hidden(piece):
+            first, count = PIECES[piece]
+            c, in_hop = divmod(first, CHUNK)
+            hid = keep.tile([P, PACK * count], BF16, name="hid%d" % first, align_bytes=64)
             nc.vector.tensor_tensor(
-                hid[:].rearrange("p (c i t) -> p c t i", i=4, t=PACK),
-                hop[c][:, :, at : at + n].rearrange("p t (c i) -> p c t i", i=4),
-                ob[:].rearrange("p t (c i) -> p c t i", i=4),
+                hid[:].rearrange("p (c q t) -> p c t q", q=RUN, t=PACK),
+                hop[c][:, :, in_hop : in_hop + count].rearrange("p t (c q) -> p c t q", q=RUN),
+                ob[piece][:].rearrange("p t (c q) -> p c t q", q=RUN),
                 ALU.subtract,
             )
             return hid
 
-        def answers(piece, hid):
-            r0, n = PIECES[piece]
-            hid_q = quantise("hid%d" % r0, hid, n)
-            for h in range(N // P):
-                bank = psum.tile([P, S], F32, name="bank%d" % ((4 + 2 * piece + h) % 8))
-                product(w4_q, h, hid_q, bank[:, :n])
-                res = keep.tile([P, n], F32, name="res%d_%d" % (r0, h))
-                if h == 0 and piece >= VFROM:
-                    nc.vector.tensor_copy(res[:], bank[:, :n])
-                else:
-                    nc.scalar.copy(res[:], bank[:, :n])
-                nc.sync.dma_start(out_v[:, h, r0 : r0 + n], res[:])
+        out_halves = out.rearrange("(h m) r -> m h r", m=P)
 
-        obs = [objects(0, "ob0"), objects(1, "ob1")]
-        hid0 = hidden(0, obs[0])
-        if EARLY < PACK:
-            hops(1, sb1, EARLY, PACK)
-        answers(0, hid0)
-        for piece in range(2, len(PIECES)):
-            obs.append(objects(piece, "hid0" if piece == HOLD else "ob%d" % piece))
-        hids = {1: hidden(1, obs[1])}
+        def answers(piece, hid):
+            first, count = PIECES[piece]
+            is_last = piece == len(PIECES) - 1
+            hid_q = quantise("hid%d" % first, hid, count)
+            for h in range(N // P):
+                acc = product(w4_q, h, hid_q, (PACK + 2 * piece + h) % BANKS)
+                result = keep.tile([P, count], F32, name="result%d_%d" % (first, h))
+                if is_last and h == 0:
+                    nc.vector.tensor_copy(result[:], acc)
+                else:
+                    nc.scalar.copy(result[:], acc)
+                nc.sync.dma_start(out_halves[:, h, first : first + count], result[:])
+
+        hids = [hidden(0)]
+        hops(sb1, 1, HOPS_BEFORE_FIRST_PIECE, PACK)
+        answers(0, hids[0])
+        hids.append(hidden(1))
         for piece in range(1, len(PIECES)):
             if piece + 1 < len(PIECES):
-                hids[piece + 1] = hidden(piece + 1, obs[piece + 1])
+                hids.append(hidden(piece + 1))
             answers(piece, hids[piece])

from contextlib import ExitStack

import concourse.mybir as mybir
from concourse.masks import make_identity

F32 = mybir.dt.float32
BF16 = mybir.dt.bfloat16
I32 = mybir.dt.int32
U32 = mybir.dt.uint32
U16 = mybir.dt.uint16
U8 = mybir.dt.uint8
FP8X4 = mybir.dt.float8_e4m3fn_x4
ALU = mybir.AluOpType
COPY = mybir.ActivationFunctionType.Copy
LAST_AXIS = mybir.AxisListType.X

P = 128
PACK = 4
RUN = 4
GROUP = PACK * RUN
K = 512
H = 512
S = 512
R = 1024
N = 256
STRIPE = 16
SPARE = 16
CHUNK = 512
BANKS = 8
PIECES = ((0, 512), (512, 256), (768, 128), (896, 128))
W1_PLANES_ON_VECTOR = 2
W3_PLANES_ON_VECTOR = 1
HOPS_BEFORE_FIRST_PIECE = 3

FLOPS = 2 * (3 * K * H * S + H * N * R)


def tile_picked_ytriple_res_p_kernel(
    tc, x_words, x_scales, w1, e_words, e_scales, w2, d_words, d_scales, w3, unit, w4,
    offs, prd, obj, ts, tp, to, out,
):
    nc = tc.nc
    with ExitStack() as ctx:
        keep = ctx.enter_context(tc.tile_pool(name="keep", bufs=1))
        ring = ctx.enter_context(tc.tile_pool(name="ring", bufs=3))
        shared = ctx.enter_context(tc.tile_pool(name="shared", bufs=1))
        psum = ctx.enter_context(tc.psum_pool(name="psum", bufs=1))

        def load_list(name, src):
            tile = keep.tile(list(src.shape), U16, name=name)
            nc.sync.dma_start(tile[:], src)
            return tile

        def load_words(name, src):
            tile = keep.tile([P, src.shape[2]], I32, name=name, align_bytes=64)
            nc.sync.dma_start(tile[:], src[0].rearrange("p n j -> p (n j)").bitcast(I32))
            return tile

        def load_scales(name, src):
            tile = keep.tile([P, src.shape[2]], U8, name=name, align_bytes=64)
            nc.vector.memset(tile[:].bitcast(I32), 0)
            rows = src[0].rearrange("(Q r) n -> r Q n", r=4)
            for r in range(4):
                nc.sync.dma_start(tile[r:P:32, :].bitcast(I32), rows[r].bitcast(I32))
            return tile

        def load_weight(name, src, c0, c1):
            tile = keep.tile([P, PACK, c1 - c0], F32, name=name, tag=name)
            nc.sync.dma_start(tile[:], src.rearrange("(p j) c -> p j c", j=PACK)[:, :, c0:c1])
            return tile

        def gather_words(picked, table, lst):
            nc.vector.tensor_copy(picked[:], table[:].bitcast(U32).indirect(lst[:]))

        def gather_scales(picked, table, lst):
            nc.vector.tensor_copy(picked[:], table[:].indirect(lst[:]))

        def gather_table(name, words, scales, lst):
            picked_words = keep.tile([P, S], U32, name=name + "_words", align_bytes=64)
            picked_scales = keep.tile([P, S], U8, name=name + "_scales", align_bytes=64)
            gather_words(picked_words, words, lst)
            gather_scales(picked_scales, scales, lst)
            return picked_words, picked_scales

        def deal_views(dealt, raw, first):
            src = raw[:].rearrange("p j (g t q) -> p t g j q", t=PACK, q=RUN)
            dst = dealt[:].rearrange("p (t g q j) -> p t g j q", t=PACK, q=RUN, j=PACK)
            return dst[:, :, first // GROUP : (first + raw.shape[2]) // GROUP], src

        def deal_on_vector(dealt, raw, first, t0, t1):
            dst, src = deal_views(dealt, raw, first)
            nc.vector.tensor_copy(dst[:, t0:t1], src[:, t0:t1])

        def deal_on_scalar(dealt, raw, first, t0, t1):
            dst, src = deal_views(dealt, raw, first)
            for t in range(t0, t1):
                nc.scalar.activation(dst[:, t], src[:, t], COPY)

        def quantise(name, values, step):
            cols = values.shape[1] // PACK
            codes = keep.tile([P, cols], U32, name=name + "_codes", align_bytes=64)
            scales = keep.tile([P, cols], U8, name=name + "_block_scales", align_bytes=64)
            for c in range(0, cols, step):
                nc.vector.quantize_mx(
                    out=codes[:, c : c + step].bitcast(FP8X4),
                    scales=scales[:, c : c + step],
                    in_=values[:, PACK * c : PACK * (c + step)],
                )
            return codes, scales

        def product(weights, block, moving, bank_number):
            cols = slice(block * P, (block + 1) * P)
            bank = psum.tile([P, S], F32, name="bank%d" % bank_number)
            acc = bank[:, : moving[0].shape[1]]
            nc.tensor.matmul_mx(
                out=acc,
                lhsT=weights[0][:, cols].bitcast(FP8X4), lhsT_scale=weights[1][:, cols],
                rhs=moving[0][:].bitcast(FP8X4), rhs_scale=moving[1][:],
                start=True, stop=True,
            )
            return acc

        def windows(name):
            tiles = [keep.tile([P, S + SPARE], F32, name="%s%d" % (name, t)) for t in range(PACK)]
            for tile in tiles:
                nc.vector.memset(tile[:, S:], 0.0)
            return tiles

        def entries(lst, first, count):
            return lst[:, first // STRIPE : (first + count) // STRIPE]

        offs_t = load_list("offs_t", offs)
        x_w = load_words("x_w", x_words)
        x_s = load_scales("x_s", x_scales)
        w1_lo = load_weight("w1_lo", w1, 0, H // 2)
        w1_hi = load_weight("w1_hi", w1, H // 2, H)
        e_w = load_words("e_w", e_words)
        prd_t = load_list("prd_t", prd)
        e_s = load_scales("e_s", e_scales)
        w2_raw = load_weight("w2_raw", w2, 0, H)
        ts_t = load_list("ts_t", ts)
        unit_group = keep.tile([P, GROUP], F32, name="unit_group")
        nc.sync.dma_start(
            unit_group[:],
            unit.rearrange("(g c) o -> g (c o)", c=GROUP).unsqueeze(1).to_broadcast([P // RUN, RUN, GROUP]),
        )
        d_w = load_words("d_w", d_words)
        d_s = load_scales("d_s", d_scales)
        obj_t = load_list("obj_t", obj)
        tp_t = load_list("tp_t", tp)
        w3_raw = load_weight("w3_raw", w3, 0, H)
        to_t = load_list("to_t", to)
        w4_raw = keep.tile([P, PACK, N], F32, name="w4_raw")
        w4_rows = w4.rearrange("(g t q) n -> t g q n", t=PACK, q=RUN)
        for t in range(PACK):
            nc.sync.dma_start(w4_raw[:, t, :], w4_rows[t])
        y, ye, yd = windows("y"), windows("ye"), windows("yd")

        eye = keep.tile([P, P], F32, name="eye")
        make_identity(nc, eye[:])
        own = keep.tile([P, RUN], F32, name="own")
        nc.vector.tensor_reduce(own[:], eye[:].rearrange("p (g q) -> p q g", q=RUN), LAST_AXIS, ALU.add)
        masked = keep.tile([P, PACK, RUN], F32, name="masked")
        nc.vector.tensor_tensor(
            masked[:],
            unit_group[:].rearrange("p (t q) -> p t q", q=RUN),
            own[:].unsqueeze(1).to_broadcast([P, PACK, RUN]),
            ALU.mult,
        )
        size = keep.tile([P, PACK], F32, name="size")
        nc.vector.tensor_reduce(size[:], masked[:], LAST_AXIS, ALU.max, apply_absolute_value=True)
        floor_factor = keep.tile([P, PACK], F32, name="floor_factor")
        nc.vector.tensor_scalar(floor_factor[:], size[:], 0.4, None, ALU.mult)
        halves = keep.tile([P, PACK, RUN // 2], F32, name="halves")
        nc.gpsimd.tensor_tensor(halves[:], masked[:, :, : RUN // 2], masked[:, :, RUN // 2 :], ALU.add)
        signed = keep.tile([P, PACK], F32, name="signed")
        nc.gpsimd.tensor_tensor(signed[:], halves[:, :, 0], halves[:, :, 1], ALU.add)
        twice_positive = keep.tile([P, PACK], F32, name="twice_positive")
        nc.gpsimd.tensor_scalar(twice_positive[:], signed[:], 0.0, 2.0, ALU.is_ge, ALU.mult)
        sign = keep.tile([P, PACK], F32, name="sign")
        nc.gpsimd.tensor_scalar(sign[:], twice_positive[:], 1.0, -1.0, ALU.mult, ALU.add)

        w1_dealt = shared.tile([P, PACK * H], BF16, name="w1_dealt", align_bytes=64, offset=0)
        deal_on_scalar(w1_dealt, w1_lo, 0, 0, PACK)
        x_picked = gather_table("x_picked", x_w, x_s, offs_t)
        deal_on_vector(w1_dealt, w1_hi, H // 2, 0, W1_PLANES_ON_VECTOR)
        deal_on_scalar(w1_dealt, w1_hi, H // 2, W1_PLANES_ON_VECTOR, PACK)
        w1_q = quantise("w1", w1_dealt, P)
        last = PACK - 1
        y_acc = [product(w1_q, t, x_picked, t) for t in range(last)]

        e_picked = (
            shared.tile([P, S], U32, name="e_picked_words", align_bytes=64, offset=0),
            shared.tile([P, S], U8, name="e_picked_scales", align_bytes=64, offset=4 * S),
        )
        gather_words(e_picked[0], e_w, prd_t)
        gather_scales(e_picked[1], e_s, prd_t)
        w2_dealt = keep.tile([P, PACK * H], BF16, name="w2_dealt", align_bytes=64)
        deal_on_vector(w2_dealt, w2_raw, 0, 0, PACK)
        w2_q = quantise("w2", w2_dealt, 2 * P)
        ye_acc = [product(w2_q, t, e_picked, last + t) for t in range(PACK)]
        d_picked = gather_table("d_picked", d_w, d_s, obj_t)

        def empty(window, acc):
            nc.scalar.activation(window[:, :S], acc, COPY)

        def empty_scaled(window, acc, t):
            nc.scalar.activation(window[:, :S], acc, COPY, scale=size[:, t : t + 1])

        def fetch_subjects(sb, c, t):
            nc.scalar.activation(sb[:, t, :], y[t][:].indirect(entries(ts_t, c * CHUNK, CHUNK)), COPY)

        def times_predicate(sb, c, t):
            prod = ring.tile([P, CHUNK], F32, name="prod")
            nc.vector.tensor_tensor(
                prod[:], ye[t][:].indirect(entries(tp_t, c * CHUNK, CHUNK)), sb[:, t, :], ALU.mult
            )
            return prod

        hop = [keep.tile([P, PACK, CHUNK], F32, name="hop%d" % c) for c in range(R // CHUNK)]

        def hops(sb, c, t0, t1):
            prods = {t0: times_predicate(sb, c, t0)}
            for t in range(t0, t1):
                if t + 1 < t1:
                    prods[t + 1] = times_predicate(sb, c, t + 1)
                nc.vector.scalar_tensor_tensor(
                    hop[c][:, t, :], sb[:, t, :], floor_factor[:, t : t + 1], prods[t][:], ALU.mult, ALU.max
                )

        sb0 = keep.tile([P, PACK, CHUNK], F32, name="sb0")
        empty(y[0], y_acc[0])
        for t in range(last):
            if t + 1 < last:
                empty(y[t + 1], y_acc[t + 1])
            fetch_subjects(sb0, 0, t)
        empty_scaled(ye[0], ye_acc[0], 0)
        y_last_acc = product(w1_q, last, x_picked, last)
        empty_scaled(ye[1], ye_acc[1], 1)
        empty(y[last], y_last_acc)
        empty_scaled(ye[2], ye_acc[2], 2)
        fetch_subjects(sb0, 0, last)
        empty_scaled(ye[3], ye_acc[3], 3)

        w3_dealt = keep.tile([P, PACK * H], BF16, name="w3_dealt", align_bytes=64)
        deal_on_vector(w3_dealt, w3_raw, 0, 0, W3_PLANES_ON_VECTOR)
        deal_on_scalar(w3_dealt, w3_raw, 0, W3_PLANES_ON_VECTOR, PACK)
        w3_q = quantise("w3", w3_dealt, H)
        yd_acc = [product(w3_q, t, d_picked, (BANKS - 1 + t) % BANKS) for t in range(PACK)]
        hops(sb0, 0, 0, PACK)

        w4_signed = keep.tile([P, PACK * N], BF16, name="w4_signed", align_bytes=64)
        nc.vector.tensor_tensor(
            w4_signed[:].rearrange("p (c q t) -> p c t q", q=RUN, t=PACK),
            w4_raw[:].rearrange("p t (c q) -> p c t q", q=RUN),
            sign[:].unsqueeze(1).unsqueeze(3).to_broadcast([P, N // RUN, PACK, RUN]),
            ALU.mult,
        )

        sb1 = keep.tile([P, PACK, CHUNK], F32, name="sb1", tag="w3_raw")
        for t in range(PACK):
            fetch_subjects(sb1, 1, t)
        for t in range(PACK):
            empty_scaled(yd[t], yd_acc[t], t)
        hops(sb1, 1, 0, HOPS_BEFORE_FIRST_PIECE)
        w4_q = quantise("w4", w4_signed, N)

        ob = []
        for first, count in PIECES:
            fetched = keep.tile([P, PACK, count], F32, name="ob%d" % first)
            for t in range(PACK):
                nc.scalar.activation(fetched[:, t, :], yd[t][:].indirect(entries(to_t, first, count)), COPY)
            ob.append(fetched)

        def hidden(piece):
            first, count = PIECES[piece]
            c, in_hop = divmod(first, CHUNK)
            hid = keep.tile([P, PACK * count], BF16, name="hid%d" % first, align_bytes=64)
            nc.vector.tensor_tensor(
                hid[:].rearrange("p (c q t) -> p c t q", q=RUN, t=PACK),
                hop[c][:, :, in_hop : in_hop + count].rearrange("p t (c q) -> p c t q", q=RUN),
                ob[piece][:].rearrange("p t (c q) -> p c t q", q=RUN),
                ALU.subtract,
            )
            return hid

        out_halves = out.rearrange("(h m) r -> m h r", m=P)

        def answers(piece, hid):
            first, count = PIECES[piece]
            is_last = piece == len(PIECES) - 1
            hid_q = quantise("hid%d" % first, hid, count)
            for h in range(N // P):
                acc = product(w4_q, h, hid_q, (PACK + 2 * piece + h) % BANKS)
                result = keep.tile([P, count], F32, name="result%d_%d" % (first, h))
                if is_last and h == 0:
                    nc.vector.tensor_copy(result[:], acc)
                else:
                    nc.scalar.copy(result[:], acc)
                nc.sync.dma_start(out_halves[:, h, first : first + count], result[:])

        hids = [hidden(0)]
        hops(sb1, 1, HOPS_BEFORE_FIRST_PIECE, PACK)
        answers(0, hids[0])
        hids.append(hidden(1))
        for piece in range(1, len(PIECES)):
            if piece + 1 < len(PIECES):
                hids.append(hidden(piece + 1))
            answers(piece, hids[piece])
